import numpy as np, ml_dtypes
CORES = [50,52,122,124]
N = 4
import mx_ref
NC = 128
BF = ml_dtypes.bfloat16
def setup_inputs(rng):
    def f(*shape):
        return mx_ref.flush((rng.standard_normal(shape, dtype=np.float32) * np.exp2(rng.integers(-2, 3, shape[:-1] + (1,)))).astype(BF))
    return {"w": f(N, 128, 512), "x": f(N, 128, 4 * NC)}
def setup_inputs_blocks(rng):
    d = setup_inputs(rng)
    for k in ("w", "x"): d[k] = mx_ref.spread(d[k], rng, 4)
    return d
def setup_inputs_wide(rng):
    d = setup_inputs(rng)
    for k in ("w", "x"): d[k] = mx_ref.flush((d[k].astype(np.float32) * np.exp2(rng.integers(-10, 11, (N, 1, 1))).astype(np.float32)).astype(BF))
    return d
def reference(w, x):
    X = [mx_ref.quantize(x[j]) for j in range(N)]
    y = np.full((N, 128, N * NC), np.nan, np.float32)
    for r in range(N):
        qw = mx_ref.quantize(w[r])
        for j in range(r + 1):
            y[r][:, NC * j:NC * j + NC] = mx_ref.matmul(qw, X[j])
    return {"y": y}

@@ -1,0 +1,140 @@
+from concourse.bass import DstId, RemoteDMATransfer
+from concourse.mybir import dt, ActivationFunctionType
+
+NC = 128
+BANK = 512
+
+SCRATCH = {
+    "xb": ("sbuf", [128, 4 * NC], "bfloat16"),
+    "wb": ("sbuf", [128, 4 * NC], "bfloat16"),
+    "xq": ("sbuf", [128, 4 * NC], "float8_e4m3fn_x4"),
+    "xs": ("sbuf", [128, 4 * NC], "uint8"),
+    "wq": ("sbuf", [128, NC], "float8_e4m3fn_x4"),
+    "ws": ("sbuf", [128, NC], "uint8"),
+    "ps": ("psum", [128, 3 * BANK], "float32"),
+    "yo": ("sbuf", [128, 4 * NC], "float32"),
+}
+SEMAPHORES = ["ldx", "ldw", "qx", "qw", "sent",
+              "s0", "c0", "s1", "c1", "s2", "c2",
+              "mm0", "mm1", "mm2", "ev0", "ev1", "ev2", "sts", "stc"]
+
+
+def _plan(cores, topo):
+    hops = []
+    for j, s in enumerate(cores):
+        need = cores[j + 1:]
+        near = [d for d in need if topo.chip(d) == topo.chip(s)]
+        far = [d for d in need if topo.chip(d) != topo.chip(s)]
+        h = {}
+        if far and all(topo.may_write(s, d) for d in far):
+            head = sorted(far, key=lambda d: topo.die(d) != topo.die(s))[0]
+            h[s] = near + [head]
+            if len(far) > 1:
+                h[head] = [d for d in far if d != head]
+        elif far:
+            gate = [c for c in cores if c != s and topo.chip(c) == topo.chip(s)
+                    and all(topo.may_write(c, d) for d in far)][0]
+            h[s] = near + [c for c in [gate] if c not in near]
+            h[gate] = far
+        elif near:
+            h[s] = near
+        hops.append(h)
+    return hops
+
+
+def _engines(m):
+    return [e for e in range(m.bit_length()) if (m >> e) & 1]
+
+
+def _masks(topo, src, dsts):
+    order = sorted(dsts, key=lambda d: len(_engines(topo.mask(src, d))))
+    used, out = [], {}
+    for i, d in enumerate(order):
+        can = [e for e in _engines(topo.mask(src, d)) if e not in used]
+        peers = len([p for p in order[i:] if topo.mask(src, p) == topo.mask(src, d)])
+        n = 1
+        while 2 * n * peers <= len(can):
+            n *= 2
+        used += can[:n]
+        out[d] = sum(1 << e for e in can[:n])
+    return out
+
+
+def rank_program(g, core, T, topo):
+    cores = list(T.cores)
+    rank = T.rank_of(core)
+    hops = _plan(cores, topo)
+    sem = T.sem
+
+    def landed(j):
+        for s, dsts in hops[j].items():
+            if core in dsts:
+                return len(_engines(_masks(topo, s, dsts)[core]))
+        return 0
+
+    jobs = sorted([j for j in range(len(cores)) if core in hops[j]], key=lambda j: (cores[j] != core, j))
+    sent = 0
+    for j in jobs:
+        dsts = hops[j][core]
+        masks = _masks(topo, core, dsts)
+        a, b = NC * j, NC * (j + 1)
+        if cores[j] == core:
+            g.wait_ge(sem.qx, 1)
+        for kind in ("s", "c"):
+            name = "%s%d" % (kind, j)
+            if cores[j] != core:
+                g.wait_ge(sem[name], landed(j))
+            transfers = []
+            for d in dsts:
+                rid, pid, _ = topo.addr(d)
+                if kind == "s":
+                    src, dst = T.xs[:, a:b], T.xs[:, a:b]
+                else:
+                    src, dst = T.xq[:, a:b].bitcast(dt.uint8), T.xq[:, a:b].bitcast(dt.uint8)
+                transfers.append(RemoteDMATransfer(dst_ids=[DstId(rid=rid, pnc=pid)], dma_engine_mask=masks[d],
+                                                   remote_sem=sem[name], src=src, dst=dst))
+                sent += len(_engines(masks[d]))
+            g.remote_dma_fused(transfers, local_sem=sem.sent)
+    if sent:
+        g.wait_ge(sem.sent, sent)
+
+    if rank is None:
+        return
+
+    a, b = NC * rank, NC * (rank + 1)
+    g.sync.dma_start(T.xb[:], T.x[:]).then_inc(sem.ldx, 16)
+    g.sync.dma_start(T.wb[:], T.w[:]).then_inc(sem.ldw, 16)
+    g.vector.wait_ge(sem.ldx, 16)
+    g.vector.quantize_mx(T.xq[:, a:b], T.xs[:, a:b], T.xb[:]).then_inc(sem.qx, 1)
+    g.vector.wait_ge(sem.ldw, 16)
+    g.vector.quantize_mx(T.wq[:], T.ws[:], T.wb[:]).then_inc(sem.qw, 1)
+
+    home = [j for j in range(rank + 1) if topo.chip(cores[j]) == topo.chip(core)]
+    groups = [home] + [[j] for j in range(rank + 1) if j not in home]
+    g.tensor.wait_ge(sem.qw, 1)
+    on_sync = 0
+    for k, grp in enumerate(groups):
+        for j in grp:
+            if j == rank:
+                g.tensor.wait_ge(sem.qx, 1)
+            else:
+                g.tensor.wait_ge(sem["s%d" % j], landed(j))
+                g.tensor.wait_ge(sem["c%d" % j], landed(j))
+        a, b = NC * grp[0], NC * (grp[-1] + 1)
+        acc = T.ps[:, BANK * k:BANK * k + (b - a)]
+        mm, ev = sem["mm%d" % k], sem["ev%d" % k]
+        g.tensor.matmul_mx(acc, T.wq[:], T.ws[:], T.xq[:, a:b], T.xs[:, a:b], True, True).then_inc(mm, 1)
+        if k == len(groups) - 1:
+            g.scalar.wait_ge(mm, 1)
+            g.scalar.activation(T.yo[:, a:b], acc, ActivationFunctionType.Copy).then_inc(ev, 1)
+            g.scalar.wait_ge(ev, 1)
+            g.scalar.dma_start(T.y[:, a:b], T.yo[:, a:b]).then_inc(sem.stc, 16)
+            g.scalar.wait_ge(sem.stc, 16)
+        else:
+            g.vector.wait_ge(mm, 1)
+            g.vector.tensor_copy(T.yo[:, a:b], acc).then_inc(ev, 1)
+            g.sync.wait_ge(ev, 1)
+            g.sync.dma_start(T.y[:, a:b], T.yo[:, a:b]).then_inc(sem.sts, 16)
+            on_sync += 16
+    if on_sync:
+        g.sync.wait_ge(sem.sts, on_sync)

@@ -19,82 +19,88 @@ SEMAPHORES = ["ldx", "ldw", "qx", "qw", "sent",
               "mm0", "mm1", "mm2", "ev0", "ev1", "ev2", "sts", "stc"]
 
 
-def _plan(cores, topo):
-    hops = []
-    for j, s in enumerate(cores):
-        need = cores[j + 1:]
-        near = [d for d in need if topo.chip(d) == topo.chip(s)]
-        far = [d for d in need if topo.chip(d) != topo.chip(s)]
-        h = {}
-        if far and all(topo.may_write(s, d) for d in far):
-            head = sorted(far, key=lambda d: topo.die(d) != topo.die(s))[0]
-            h[s] = near + [head]
-            if len(far) > 1:
-                h[head] = [d for d in far if d != head]
-        elif far:
-            gate = [c for c in cores if c != s and topo.chip(c) == topo.chip(s)
-                    and all(topo.may_write(c, d) for d in far)][0]
-            h[s] = near + [c for c in [gate] if c not in near]
-            h[gate] = far
-        elif near:
-            h[s] = near
-        hops.append(h)
-    return hops
-
-
 def _engines(m):
     return [e for e in range(m.bit_length()) if (m >> e) & 1]
 
 
-def _masks(topo, src, dsts):
-    order = sorted(dsts, key=lambda d: len(_engines(topo.mask(src, d))))
-    used, out = [], {}
-    for i, d in enumerate(order):
-        can = [e for e in _engines(topo.mask(src, d)) if e not in used]
-        peers = len([p for p in order[i:] if topo.mask(src, p) == topo.mask(src, d)])
-        n = 1
-        while 2 * n * peers <= len(can):
-            n *= 2
-        used += can[:n]
-        out[d] = sum(1 << e for e in can[:n])
-    return out
+def _bits(es):
+    return sum(1 << e for e in es)
+
+
+def _sends(cores, topo, ncores):
+    own, late = {}, {}
+
+    def add(book, s, j, kind, writes):
+        book.setdefault(s, []).append((j, kind, writes))
+
+    for j, s in enumerate(cores):
+        a, b = NC * j, NC * (j + 1)
+        near = [d for d in cores[j + 1:] if topo.chip(d) == topo.chip(s)]
+        far = [d for d in cores[j + 1:] if topo.chip(d) != topo.chip(s)]
+        used = []
+        if far and all(topo.may_write(s, d) for d in far):
+            head = sorted(far, key=lambda d: topo.die(d) != topo.die(s))[0]
+            used = _engines(topo.mask(s, head))
+            for kind in "sc":
+                add(own, s, j, kind, [(head, _bits(used), a, b)])
+                for d in far:
+                    if d != head:
+                        add(late, head, j, kind, [(d, topo.mask(head, d), a, b)])
+        elif far:
+            mates = [c for c in range(ncores) if c != s and topo.chip(c) == topo.chip(s)
+                     and all(topo.may_write(c, d) for d in far)]
+            gate = [c for c in mates if c in cores][0]
+            relays = [c for c in mates if c not in cores and topo.die(c) == topo.die(s)][:2]
+            first = sorted(far, key=lambda d: topo.die(d) != topo.die(gate))[0]
+            other = [d for d in far if d != first][0]
+            eng = _engines(topo.mask(s, gate))
+            one, two = eng[::2], eng[1::2]
+            off = _engines(topo.mask(gate, first))
+            h, k, m = len(one) // 2, len(off) // 2, (a + b) // 2
+            add(own, s, j, "c", [(relays[0], _bits(one[:h]), a, m), (relays[1], _bits(one[h:]), m, b)])
+            add(own, s, j, "s", [(gate, _bits(two), a, b)])
+            add(own, s, j, "c", [(gate, _bits(two), a, b)])
+            add(late, gate, j, "s", [(first, _bits(off[:k]), a, b), (other, _bits(off[k:]), a, b)])
+            add(late, gate, j, "c", [(first, _bits(off), a, b)])
+            add(late, relays[0], j, "c", [(other, topo.mask(relays[0], other), a, m)])
+            add(late, relays[1], j, "c", [(other, topo.mask(relays[1], other), m, b)])
+        for d in near:
+            rest = [e for e in _engines(topo.mask(s, d)) if e not in used]
+            for kind in "sc":
+                add(own, s, j, kind, [(d, _bits(rest), a, b)])
+    return {s: own.get(s, []) + late.get(s, []) for s in list(own) + list(late)}
 
 
 def rank_program(g, core, T, topo):
     cores = list(T.cores)
     rank = T.rank_of(core)
-    hops = _plan(cores, topo)
     sem = T.sem
+    sends = _sends(cores, topo, topo.CHIPS * topo.CORES_PER_CHIP)
 
-    def landed(j):
-        for s, dsts in hops[j].items():
-            if core in dsts:
-                return len(_engines(_masks(topo, s, dsts)[core]))
-        return 0
+    def landed(name):
+        return sum(len(_engines(m)) for calls in sends.values() for j, kind, writes in calls
+                   for d, m, a, b in writes if d == core and "%s%d" % (kind, j) == name)
 
-    jobs = sorted([j for j in range(len(cores)) if core in hops[j]], key=lambda j: (cores[j] != core, j))
     sent = 0
-    for j in jobs:
-        dsts = hops[j][core]
-        masks = _masks(topo, core, dsts)
-        a, b = NC * j, NC * (j + 1)
+    gate = False
+    for j, kind, writes in sends.get(core, []):
+        name = "%s%d" % (kind, j)
         if cores[j] == core:
             g.wait_ge(sem.qx, 1)
-        for kind in ("s", "c"):
-            name = "%s%d" % (kind, j)
-            if cores[j] != core:
-                g.wait_ge(sem[name], landed(j))
-            transfers = []
-            for d in dsts:
-                rid, pid, _ = topo.addr(d)
-                if kind == "s":
-                    src, dst = T.xs[:, a:b], T.xs[:, a:b]
-                else:
-                    src, dst = T.xq[:, a:b].bitcast(dt.uint8), T.xq[:, a:b].bitcast(dt.uint8)
-                transfers.append(RemoteDMATransfer(dst_ids=[DstId(rid=rid, pnc=pid)], dma_engine_mask=masks[d],
-                                                   remote_sem=sem[name], src=src, dst=dst))
-                sent += len(_engines(masks[d]))
-            g.remote_dma_fused(transfers, local_sem=sem.sent)
+        else:
+            g.wait_ge(sem[name], landed(name))
+            gate = gate or any(topo.chip(d) != topo.chip(core) for d, m, a, b in writes)
+        transfers = []
+        for d, m, a, b in writes:
+            rid, pid, _ = topo.addr(d)
+            if kind == "s":
+                src, dst = T.xs[:, a:b], T.xs[:, a:b]
+            else:
+                src, dst = T.xq[:, a:b].bitcast(dt.uint8), T.xq[:, a:b].bitcast(dt.uint8)
+            transfers.append(RemoteDMATransfer(dst_ids=[DstId(rid=rid, pnc=pid)], dma_engine_mask=m,
+                                               remote_sem=sem[name], src=src, dst=dst))
+            sent += len(_engines(m))
+        g.remote_dma_fused(transfers, local_sem=sem.sent)
     if sent:
         g.wait_ge(sem.sent, sent)
 
@@ -118,8 +124,8 @@ def rank_program(g, core, T, topo):
             if j == rank:
                 g.tensor.wait_ge(sem.qx, 1)
             else:
-                g.tensor.wait_ge(sem["s%d" % j], landed(j))
-                g.tensor.wait_ge(sem["c%d" % j], landed(j))
+                g.tensor.wait_ge(sem["s%d" % j], landed("s%d" % j))
+                g.tensor.wait_ge(sem["c%d" % j], landed("c%d" % j))
         a, b = NC * grp[0], NC * (grp[-1] + 1)
         acc = T.ps[:, BANK * k:BANK * k + (b - a)]
         mm, ev = sem["mm%d" % k], sem["ev%d" % k]
@@ -128,6 +134,8 @@ def rank_program(g, core, T, topo):
             g.scalar.wait_ge(mm, 1)
             g.scalar.activation(T.yo[:, a:b], acc, ActivationFunctionType.Copy).then_inc(ev, 1)
             g.scalar.wait_ge(ev, 1)
+            if gate:
+                g.scalar.wait_ge(sem.sent, sent)
             g.scalar.dma_start(T.y[:, a:b], T.yo[:, a:b]).then_inc(sem.stc, 16)
             g.scalar.wait_ge(sem.stc, 16)
         else:

from concourse.bass import DstId, RemoteDMATransfer
from concourse.mybir import dt, ActivationFunctionType

NC = 128
BANK = 512

SCRATCH = {
    "xb": ("sbuf", [128, 4 * NC], "bfloat16"),
    "wb": ("sbuf", [128, 4 * NC], "bfloat16"),
    "xq": ("sbuf", [128, 4 * NC], "float8_e4m3fn_x4"),
    "xs": ("sbuf", [128, 4 * NC], "uint8"),
    "wq": ("sbuf", [128, NC], "float8_e4m3fn_x4"),
    "ws": ("sbuf", [128, NC], "uint8"),
    "ps": ("psum", [128, 3 * BANK], "float32"),
    "yo": ("sbuf", [128, 4 * NC], "float32"),
}
SEMAPHORES = ["ldx", "ldw", "qx", "qw", "sent",
              "s0", "c0", "s1", "c1", "s2", "c2",
              "mm0", "mm1", "mm2", "ev0", "ev1", "ev2", "sts", "stc"]


def _engines(m):
    return [e for e in range(m.bit_length()) if (m >> e) & 1]


def _bits(es):
    return sum(1 << e for e in es)


def _sends(cores, topo, ncores):
    own, late = {}, {}

    def add(book, s, j, kind, writes):
        book.setdefault(s, []).append((j, kind, writes))

    for j, s in enumerate(cores):
        a, b = NC * j, NC * (j + 1)
        near = [d for d in cores[j + 1:] if topo.chip(d) == topo.chip(s)]
        far = [d for d in cores[j + 1:] if topo.chip(d) != topo.chip(s)]
        used = []
        if far and all(topo.may_write(s, d) for d in far):
            head = sorted(far, key=lambda d: topo.die(d) != topo.die(s))[0]
            used = _engines(topo.mask(s, head))
            for kind in "sc":
                add(own, s, j, kind, [(head, _bits(used), a, b)])
                for d in far:
                    if d != head:
                        add(late, head, j, kind, [(d, topo.mask(head, d), a, b)])
        elif far:
            mates = [c for c in range(ncores) if c != s and topo.chip(c) == topo.chip(s)
                     and all(topo.may_write(c, d) for d in far)]
            gate = [c for c in mates if c in cores][0]
            relays = [c for c in mates if c not in cores and topo.die(c) == topo.die(s)][:2]
            first = sorted(far, key=lambda d: topo.die(d) != topo.die(gate))[0]
            other = [d for d in far if d != first][0]
            eng = _engines(topo.mask(s, gate))
            one, two = eng[::2], eng[1::2]
            off = _engines(topo.mask(gate, first))
            h, k, m = len(one) // 2, len(off) // 2, (a + b) // 2
            add(own, s, j, "c", [(relays[0], _bits(one[:h]), a, m), (relays[1], _bits(one[h:]), m, b)])
            add(own, s, j, "s", [(gate, _bits(two), a, b)])
            add(own, s, j, "c", [(gate, _bits(two), a, b)])
            add(late, gate, j, "s", [(first, _bits(off[:k]), a, b), (other, _bits(off[k:]), a, b)])
            add(late, gate, j, "c", [(first, _bits(off), a, b)])
            add(late, relays[0], j, "c", [(other, topo.mask(relays[0], other), a, m)])
            add(late, relays[1], j, "c", [(other, topo.mask(relays[1], other), m, b)])
        for d in near:
            rest = [e for e in _engines(topo.mask(s, d)) if e not in used]
            for kind in "sc":
                add(own, s, j, kind, [(d, _bits(rest), a, b)])
    return {s: own.get(s, []) + late.get(s, []) for s in list(own) + list(late)}


def rank_program(g, core, T, topo):
    cores = list(T.cores)
    rank = T.rank_of(core)
    sem = T.sem
    sends = _sends(cores, topo, topo.CHIPS * topo.CORES_PER_CHIP)

    def landed(name):
        return sum(len(_engines(m)) for calls in sends.values() for j, kind, writes in calls
                   for d, m, a, b in writes if d == core and "%s%d" % (kind, j) == name)

    sent = 0
    gate = False
    for j, kind, writes in sends.get(core, []):
        name = "%s%d" % (kind, j)
        if cores[j] == core:
            g.wait_ge(sem.qx, 1)
        else:
            g.wait_ge(sem[name], landed(name))
            gate = gate or any(topo.chip(d) != topo.chip(core) for d, m, a, b in writes)
        transfers = []
        for d, m, a, b in writes:
            rid, pid, _ = topo.addr(d)
            if kind == "s":
                src, dst = T.xs[:, a:b], T.xs[:, a:b]
            else:
                src, dst = T.xq[:, a:b].bitcast(dt.uint8), T.xq[:, a:b].bitcast(dt.uint8)
            transfers.append(RemoteDMATransfer(dst_ids=[DstId(rid=rid, pnc=pid)], dma_engine_mask=m,
                                               remote_sem=sem[name], src=src, dst=dst))
            sent += len(_engines(m))
        g.remote_dma_fused(transfers, local_sem=sem.sent)
    if sent:
        g.wait_ge(sem.sent, sent)

    if rank is None:
        return

    a, b = NC * rank, NC * (rank + 1)
    g.sync.dma_start(T.xb[:], T.x[:]).then_inc(sem.ldx, 16)
    g.sync.dma_start(T.wb[:], T.w[:]).then_inc(sem.ldw, 16)
    g.vector.wait_ge(sem.ldx, 16)
    g.vector.quantize_mx(T.xq[:, a:b], T.xs[:, a:b], T.xb[:]).then_inc(sem.qx, 1)
    g.vector.wait_ge(sem.ldw, 16)
    g.vector.quantize_mx(T.wq[:], T.ws[:], T.wb[:]).then_inc(sem.qw, 1)

    home = [j for j in range(rank + 1) if topo.chip(cores[j]) == topo.chip(core)]
    groups = [home] + [[j] for j in range(rank + 1) if j not in home]
    g.tensor.wait_ge(sem.qw, 1)
    on_sync = 0
    for k, grp in enumerate(groups):
        for j in grp:
            if j == rank:
                g.tensor.wait_ge(sem.qx, 1)
            else:
                g.tensor.wait_ge(sem["s%d" % j], landed("s%d" % j))
                g.tensor.wait_ge(sem["c%d" % j], landed("c%d" % j))
        a, b = NC * grp[0], NC * (grp[-1] + 1)
        acc = T.ps[:, BANK * k:BANK * k + (b - a)]
        mm, ev = sem["mm%d" % k], sem["ev%d" % k]
        g.tensor.matmul_mx(acc, T.wq[:], T.ws[:], T.xq[:, a:b], T.xs[:, a:b], True, True).then_inc(mm, 1)
        if k == len(groups) - 1:
            g.scalar.wait_ge(mm, 1)
            g.scalar.activation(T.yo[:, a:b], acc, ActivationFunctionType.Copy).then_inc(ev, 1)
            g.scalar.wait_ge(ev, 1)
            if gate:
                g.scalar.wait_ge(sem.sent, sent)
            g.scalar.dma_start(T.y[:, a:b], T.yo[:, a:b]).then_inc(sem.stc, 16)
            g.scalar.wait_ge(sem.stc, 16)
        else:
            g.vector.wait_ge(mm, 1)
            g.vector.tensor_copy(T.yo[:, a:b], acc).then_inc(ev, 1)
            g.sync.wait_ge(ev, 1)
            g.sync.dma_start(T.y[:, a:b], T.yo[:, a:b]).then_inc(sem.sts, 16)
            on_sync += 16
    if on_sync:
        g.sync.wait_ge(sem.sts, on_sync)
